import numpy as np
CORES = [14,30,46,62,78,94,110,126,6,22,38,54,70,86,102,118]
N = 16
def setup_inputs(rng):
    return {"x1": rng.standard_normal((N, 128, 16), dtype=np.float32), "x2": rng.standard_normal((N, 128, 128), dtype=np.float32)}
def reference(x1, x2):
    out = []
    s = x1.sum(axis=0, dtype=np.float64).astype(x1.dtype)
    b = 16 // N
    out.append(np.stack([s[:, r * b:(r + 1) * b] for r in range(N)]))
    g = np.concatenate(list(x2), axis=1)
    out.append(np.broadcast_to(g, (N,) + g.shape))
    return {"y1": out[0], "y2": out[1]}

@@ -1,0 +1,80 @@
+from concourse.bass import DstId, RemoteDMATransfer
+from concourse.mybir import AluOpType
+
+SCRATCH = {
+    "x1s": ("sbuf", [128, 16], "float32"),
+    "land1": ("sbuf", [128, 16], "float32"),
+    "gath": ("sbuf", [128, 2048], "float32"),
+}
+SEMAPHORES = ["ld1", "ld2", "cp1", "a1", "a2p", "a2m", "acc", "sent", "st2"]
+
+
+def rank_program(g, core, T, topo):
+    r = T.rank_of(core)
+    if r is None:
+        return
+    S = T.sem
+    cores = T.cores
+    n = 16
+
+    def did(c):
+        rid, pid, _se = topo.addr(c)
+        return DstId(rid=rid, pnc=pid)
+
+    def blk(j):
+        return slice(128 * j, 128 * (j + 1))
+
+    my_chip = topo.chip(core)
+    plane = [j for j in range(n) if j != r and topo.same_plane(my_chip, topo.chip(cores[j]))]
+    mate = [j for j in range(n) if topo.mates(my_chip, topo.chip(cores[j]))][0]
+    h0 = (r // 8) * 1024
+    o0 = 1024 - h0
+
+    g.sync.dma_start(T.x1s[:], T.x1[:]).then_inc(S.ld1, 16)
+    g.scalar.dma_start(T.gath[:, blk(r)], T.x2[:]).then_inc(S.ld2, 16)
+    g.sync.wait_ge(S.ld1, 16)
+    g.sync.dma_start(T.land1[:, r:r + 1], T.x1s[:, r:r + 1]).then_inc(S.cp1, 16)
+
+    g.wait_ge(S.ld1, 16)
+    others = [j for j in range(n) if j != r]
+    sent = 0
+    for part in (others[:8], others[8:]):
+        trs = []
+        for e, j in enumerate(part):
+            trs.append(RemoteDMATransfer(dst_ids=[did(cores[j])], dma_engine_mask=1 << e, remote_sem=S.a1,
+                                         src=T.x1s[:, j:j + 1], dst=T.land1[:, r:r + 1]))
+            sent += 1
+        g.remote_dma_fused(trs, local_sem=S.sent)
+
+    g.wait_ge(S.ld2, 16)
+    g.remote_dma_fused([RemoteDMATransfer(dst_ids=[did(cores[j]) for j in plane], dma_engine_mask=0xFF,
+                                          remote_sem=S.a2p, srcs=[T.gath[:, blk(r)]],
+                                          dsts=[T.gath[:, blk(r)] for _j in plane])], local_sem=S.sent)
+    sent += 8
+
+    g.wait_ge(S.a2p, 56)
+    rid, pid, _se = topo.addr(cores[mate])
+    g.remote_dma(T.gath[:, h0:h0 + 1024], T.gath[:, h0:h0 + 1024], S.a2m, S.sent, pid, rid, 0xFF)
+    sent += 8
+
+    g.sync.wait_ge(S.ld2, 16)
+    g.sync.wait_ge(S.a2p, 56)
+    g.sync.dma_start(T.y2[:, h0:h0 + 1024], T.gath[:, h0:h0 + 1024]).then_inc(S.st2, 16)
+    g.scalar.wait_ge(S.a2m, 8)
+    g.scalar.dma_start(T.y2[:, o0:o0 + 1024], T.gath[:, o0:o0 + 1024]).then_inc(S.st2, 16)
+
+    g.wait_ge(S.a1, 15)
+    g.wait_ge(S.cp1, 16)
+    k = 0
+    w = 8
+    while w >= 1:
+        g.dma_start(T.land1[:, 0:w], T.land1[:, w:2 * w], accum_op=AluOpType.add).then_inc(S.acc, 16)
+        k += 16
+        g.wait_ge(S.acc, k)
+        w //= 2
+    g.dma_start(T.y1[:], T.land1[:, 0:1]).then_inc(S.acc, 16)
+    k += 16
+    g.wait_ge(S.acc, k)
+
+    g.wait_ge(S.sent, sent)
+    g.wait_ge(S.st2, 32)

@@ -1,80 +1,110 @@
 from concourse.bass import DstId, RemoteDMATransfer
-from concourse.mybir import AluOpType
 
 SCRATCH = {
-    "x1s": ("sbuf", [128, 16], "float32"),
-    "land1": ("sbuf", [128, 16], "float32"),
     "gath": ("sbuf", [128, 2048], "float32"),
+    "stage": ("sbuf", [128, 128], "float32"),
+    "pq": ("sbuf", [128, 512], "float32"),
+    "xd": ("dram", [8, 128, 2], "float32"),
+    "al": ("dram", [8, 128, 2], "float32"),
+    "bl": ("dram", [4, 128, 2], "float32"),
+    "sfull": ("dram", [8, 128, 2], "float32"),
 }
-SEMAPHORES = ["ld1", "ld2", "cp1", "a1", "a2p", "a2m", "acc", "sent", "st2"]
+SEMAPHORES = ["ld1", "ld2", "aq", "ap", "am", "amp", "p_st", "p_in", "a_in", "b_in", "s_in", "ex", "sent", "st2"]
+
+P2_K, P3_K, A_K, B_K = 2, 3, 7, 5
+OFF = 0x00FF
+ONLY_ON = 0xFF00
 
 
 def rank_program(g, core, T, topo):
-    r = T.rank_of(core)
-    if r is None:
-        return
     S = T.sem
     cores = T.cores
-    n = 16
+    rank_on_chip = {topo.chip(c): j for j, c in enumerate(cores)}
+    r = rank_on_chip[topo.chip(core)]
+    pl, i = divmod(r, 8)
+    m = r ^ 8
+    q_mine, q_other = r // 4, (r // 4) ^ 1
 
     def did(c):
         rid, pid, _se = topo.addr(c)
         return DstId(rid=rid, pnc=pid)
 
+    def helper(j, k):
+        return did(topo.chip(cores[j]) * 8 + k)
+
     def blk(j):
         return slice(128 * j, 128 * (j + 1))
 
-    my_chip = topo.chip(core)
-    plane = [j for j in range(n) if j != r and topo.same_plane(my_chip, topo.chip(cores[j]))]
-    mate = [j for j in range(n) if topo.mates(my_chip, topo.chip(cores[j]))][0]
-    h0 = (r // 8) * 1024
-    o0 = 1024 - h0
+    def quad(q):
+        return slice(512 * q, 512 * (q + 1))
 
-    g.sync.dma_start(T.x1s[:], T.x1[:]).then_inc(S.ld1, 16)
-    g.scalar.dma_start(T.gath[:, blk(r)], T.x2[:]).then_inc(S.ld2, 16)
-    g.sync.wait_ge(S.ld1, 16)
-    g.sync.dma_start(T.land1[:, r:r + 1], T.x1s[:, r:r + 1]).then_inc(S.cp1, 16)
+    k = core % 8
 
-    g.wait_ge(S.ld1, 16)
-    others = [j for j in range(n) if j != r]
-    sent = 0
-    for part in (others[:8], others[8:]):
-        trs = []
-        for e, j in enumerate(part):
-            trs.append(RemoteDMATransfer(dst_ids=[did(cores[j])], dma_engine_mask=1 << e, remote_sem=S.a1,
-                                         src=T.x1s[:, j:j + 1], dst=T.land1[:, r:r + 1]))
-            sent += 1
-        g.remote_dma_fused(trs, local_sem=S.sent)
+    if T.rank_of(core) is not None:
+        g.sync.dma_start(T.xd[:], T.x1[:]).then_inc(S.ld1, 16)
+        g.scalar.dma_start(T.gath[:, blk(r)], T.x2[:]).then_inc(S.ld2, 16)
 
-    g.wait_ge(S.ld2, 16)
-    g.remote_dma_fused([RemoteDMATransfer(dst_ids=[did(cores[j]) for j in plane], dma_engine_mask=0xFF,
-                                          remote_sem=S.a2p, srcs=[T.gath[:, blk(r)]],
-                                          dsts=[T.gath[:, blk(r)] for _j in plane])], local_sem=S.sent)
-    sent += 8
+        g.wait_ge(S.ld1, 16)
+        g.remote_dma_fused([RemoteDMATransfer(dst_ids=[helper(8 * pl + t, A_K)], dma_engine_mask=1 << t,
+                                              remote_sem=S.a_in, src=T.xd[t], dst=T.al[i]) for t in range(8)],
+                           local_sem=S.sent)
+        peers = [j for j in range(4 * q_mine, 4 * q_mine + 4) if j != r]
+        g.wait_ge(S.ld2, 16)
+        g.remote_dma_fused([
+            RemoteDMATransfer(dst_ids=[helper(r, P2_K)], dma_engine_mask=ONLY_ON, remote_sem=S.p_st,
+                              src=T.gath[:, blk(r)], dst=T.stage[:]),
+            RemoteDMATransfer(dst_ids=[did(cores[j]) for j in peers], dma_engine_mask=OFF, remote_sem=S.aq,
+                              srcs=[T.gath[:, blk(r)]], dsts=[T.gath[:, blk(r)] for _j in peers]),
+        ], local_sem=S.sent)
+        g.wait_ge(S.aq, 24)
+        rid, pid, _se = topo.addr(cores[m])
+        g.remote_dma(T.gath[:, quad(q_mine)], T.gath[:, quad(q_mine)], S.am, S.sent, pid, rid, OFF)
 
-    g.wait_ge(S.a2p, 56)
-    rid, pid, _se = topo.addr(cores[mate])
-    g.remote_dma(T.gath[:, h0:h0 + 1024], T.gath[:, h0:h0 + 1024], S.a2m, S.sent, pid, rid, 0xFF)
-    sent += 8
+        g.sync.wait_ge(S.ld2, 16)
+        g.sync.wait_ge(S.aq, 24)
+        g.sync.dma_start(T.y2[:, quad(q_mine)], T.gath[:, quad(q_mine)]).then_inc(S.st2, 16)
+        g.scalar.wait_ge(S.am, 8)
+        g.scalar.dma_start(T.y2[:, quad(m // 4)], T.gath[:, quad(m // 4)]).then_inc(S.st2, 16)
+        g.sync.wait_ge(S.ap, 8)
+        g.sync.dma_start(T.y2[:, quad(q_other)], T.gath[:, quad(q_other)]).then_inc(S.st2, 16)
+        g.scalar.wait_ge(S.amp, 8)
+        g.scalar.dma_start(T.y2[:, quad((m // 4) ^ 1)], T.gath[:, quad((m // 4) ^ 1)]).then_inc(S.st2, 16)
 
-    g.sync.wait_ge(S.ld2, 16)
-    g.sync.wait_ge(S.a2p, 56)
-    g.sync.dma_start(T.y2[:, h0:h0 + 1024], T.gath[:, h0:h0 + 1024]).then_inc(S.st2, 16)
-    g.scalar.wait_ge(S.a2m, 8)
-    g.scalar.dma_start(T.y2[:, o0:o0 + 1024], T.gath[:, o0:o0 + 1024]).then_inc(S.st2, 16)
+        g.wait_ge(S.s_in, 64)
+        g.dma_start(T.y1[:], T.sfull[:, r // 2::8, r % 2], allow_slow_non_contiguous=True).then_inc(S.ex, 16)
+        g.wait_ge(S.ex, 16)
+        g.wait_ge(S.sent, 8 + 16 + 8)
+        g.wait_ge(S.st2, 64)
 
-    g.wait_ge(S.a1, 15)
-    g.wait_ge(S.cp1, 16)
-    k = 0
-    w = 8
-    while w >= 1:
-        g.dma_start(T.land1[:, 0:w], T.land1[:, w:2 * w], accum_op=AluOpType.add).then_inc(S.acc, 16)
-        k += 16
-        g.wait_ge(S.acc, k)
-        w //= 2
-    g.dma_start(T.y1[:], T.land1[:, 0:1]).then_inc(S.acc, 16)
-    k += 16
-    g.wait_ge(S.acc, k)
+    elif k == P2_K:
+        far = range(4 * q_other, 4 * q_other + 4)
+        g.wait_ge(S.p_st, 8)
+        g.remote_dma_fused([RemoteDMATransfer(dst_ids=[helper(j, P3_K) for j in far], dma_engine_mask=OFF,
+                                              remote_sem=S.p_in, srcs=[T.stage[:]],
+                                              dsts=[T.pq[:, blk(r % 4)] for _j in far])], local_sem=S.sent)
+        g.wait_ge(S.sent, 8)
 
-    g.wait_ge(S.sent, sent)
-    g.wait_ge(S.st2, 32)
+    elif k == P3_K:
+        g.wait_ge(S.p_in, 32)
+        g.remote_dma_fused([
+            RemoteDMATransfer(dst_ids=[did(cores[r])], dma_engine_mask=ONLY_ON, remote_sem=S.ap,
+                              src=T.pq[:], dst=T.gath[:, quad(q_other)]),
+            RemoteDMATransfer(dst_ids=[did(cores[m])], dma_engine_mask=OFF, remote_sem=S.amp,
+                              src=T.pq[:], dst=T.gath[:, quad(q_other)]),
+        ], local_sem=S.sent)
+        g.wait_ge(S.sent, 16)
+
+    elif k == A_K:
+        g.wait_ge(S.a_in, 8)
+        g.remote_dma_fused([RemoteDMATransfer(dst_ids=[helper(r, B_K), helper(m, B_K)], dma_engine_mask=0xF << (4 * h),
+                                              remote_sem=S.b_in, srcs=[T.al[4 * h + t] for t in range(4)],
+                                              dsts=[T.bl[2 * pl + h], T.bl[2 * pl + h]], alu_op=1)
+                            for h in range(2)], local_sem=S.sent)
+        g.wait_ge(S.sent, 8)
+
+    elif k == B_K:
+        g.wait_ge(S.b_in, 16)
+        g.remote_dma_fused([RemoteDMATransfer(dst_ids=[did(cores[8 * pl + t]) for t in range(8)], dma_engine_mask=OFF,
+                                              remote_sem=S.s_in, srcs=[T.bl[t] for t in range(4)],
+                                              dsts=[T.sfull[i] for _t in range(8)], alu_op=1)], local_sem=S.sent)
+        g.wait_ge(S.sent, 8)

from concourse.bass import DstId, RemoteDMATransfer

SCRATCH = {
    "gath": ("sbuf", [128, 2048], "float32"),
    "stage": ("sbuf", [128, 128], "float32"),
    "pq": ("sbuf", [128, 512], "float32"),
    "xd": ("dram", [8, 128, 2], "float32"),
    "al": ("dram", [8, 128, 2], "float32"),
    "bl": ("dram", [4, 128, 2], "float32"),
    "sfull": ("dram", [8, 128, 2], "float32"),
}
SEMAPHORES = ["ld1", "ld2", "aq", "ap", "am", "amp", "p_st", "p_in", "a_in", "b_in", "s_in", "ex", "sent", "st2"]

P2_K, P3_K, A_K, B_K = 2, 3, 7, 5
OFF = 0x00FF
ONLY_ON = 0xFF00


def rank_program(g, core, T, topo):
    S = T.sem
    cores = T.cores
    rank_on_chip = {topo.chip(c): j for j, c in enumerate(cores)}
    r = rank_on_chip[topo.chip(core)]
    pl, i = divmod(r, 8)
    m = r ^ 8
    q_mine, q_other = r // 4, (r // 4) ^ 1

    def did(c):
        rid, pid, _se = topo.addr(c)
        return DstId(rid=rid, pnc=pid)

    def helper(j, k):
        return did(topo.chip(cores[j]) * 8 + k)

    def blk(j):
        return slice(128 * j, 128 * (j + 1))

    def quad(q):
        return slice(512 * q, 512 * (q + 1))

    k = core % 8

    if T.rank_of(core) is not None:
        g.sync.dma_start(T.xd[:], T.x1[:]).then_inc(S.ld1, 16)
        g.scalar.dma_start(T.gath[:, blk(r)], T.x2[:]).then_inc(S.ld2, 16)

        g.wait_ge(S.ld1, 16)
        g.remote_dma_fused([RemoteDMATransfer(dst_ids=[helper(8 * pl + t, A_K)], dma_engine_mask=1 << t,
                                              remote_sem=S.a_in, src=T.xd[t], dst=T.al[i]) for t in range(8)],
                           local_sem=S.sent)
        peers = [j for j in range(4 * q_mine, 4 * q_mine + 4) if j != r]
        g.wait_ge(S.ld2, 16)
        g.remote_dma_fused([
            RemoteDMATransfer(dst_ids=[helper(r, P2_K)], dma_engine_mask=ONLY_ON, remote_sem=S.p_st,
                              src=T.gath[:, blk(r)], dst=T.stage[:]),
            RemoteDMATransfer(dst_ids=[did(cores[j]) for j in peers], dma_engine_mask=OFF, remote_sem=S.aq,
                              srcs=[T.gath[:, blk(r)]], dsts=[T.gath[:, blk(r)] for _j in peers]),
        ], local_sem=S.sent)
        g.wait_ge(S.aq, 24)
        rid, pid, _se = topo.addr(cores[m])
        g.remote_dma(T.gath[:, quad(q_mine)], T.gath[:, quad(q_mine)], S.am, S.sent, pid, rid, OFF)

        g.sync.wait_ge(S.ld2, 16)
        g.sync.wait_ge(S.aq, 24)
        g.sync.dma_start(T.y2[:, quad(q_mine)], T.gath[:, quad(q_mine)]).then_inc(S.st2, 16)
        g.scalar.wait_ge(S.am, 8)
        g.scalar.dma_start(T.y2[:, quad(m // 4)], T.gath[:, quad(m // 4)]).then_inc(S.st2, 16)
        g.sync.wait_ge(S.ap, 8)
        g.sync.dma_start(T.y2[:, quad(q_other)], T.gath[:, quad(q_other)]).then_inc(S.st2, 16)
        g.scalar.wait_ge(S.amp, 8)
        g.scalar.dma_start(T.y2[:, quad((m // 4) ^ 1)], T.gath[:, quad((m // 4) ^ 1)]).then_inc(S.st2, 16)

        g.wait_ge(S.s_in, 64)
        g.dma_start(T.y1[:], T.sfull[:, r // 2::8, r % 2], allow_slow_non_contiguous=True).then_inc(S.ex, 16)
        g.wait_ge(S.ex, 16)
        g.wait_ge(S.sent, 8 + 16 + 8)
        g.wait_ge(S.st2, 64)

    elif k == P2_K:
        far = range(4 * q_other, 4 * q_other + 4)
        g.wait_ge(S.p_st, 8)
        g.remote_dma_fused([RemoteDMATransfer(dst_ids=[helper(j, P3_K) for j in far], dma_engine_mask=OFF,
                                              remote_sem=S.p_in, srcs=[T.stage[:]],
                                              dsts=[T.pq[:, blk(r % 4)] for _j in far])], local_sem=S.sent)
        g.wait_ge(S.sent, 8)

    elif k == P3_K:
        g.wait_ge(S.p_in, 32)
        g.remote_dma_fused([
            RemoteDMATransfer(dst_ids=[did(cores[r])], dma_engine_mask=ONLY_ON, remote_sem=S.ap,
                              src=T.pq[:], dst=T.gath[:, quad(q_other)]),
            RemoteDMATransfer(dst_ids=[did(cores[m])], dma_engine_mask=OFF, remote_sem=S.amp,
                              src=T.pq[:], dst=T.gath[:, quad(q_other)]),
        ], local_sem=S.sent)
        g.wait_ge(S.sent, 16)

    elif k == A_K:
        g.wait_ge(S.a_in, 8)
        g.remote_dma_fused([RemoteDMATransfer(dst_ids=[helper(r, B_K), helper(m, B_K)], dma_engine_mask=0xF << (4 * h),
                                              remote_sem=S.b_in, srcs=[T.al[4 * h + t] for t in range(4)],
                                              dsts=[T.bl[2 * pl + h], T.bl[2 * pl + h]], alu_op=1)
                            for h in range(2)], local_sem=S.sent)
        g.wait_ge(S.sent, 8)

    elif k == B_K:
        g.wait_ge(S.b_in, 16)
        g.remote_dma_fused([RemoteDMATransfer(dst_ids=[did(cores[8 * pl + t]) for t in range(8)], dma_engine_mask=OFF,
                                              remote_sem=S.s_in, srcs=[T.bl[t] for t in range(4)],
                                              dsts=[T.sfull[i] for _t in range(8)], alu_op=1)], local_sem=S.sent)
        g.wait_ge(S.sent, 8)
